import numpy as np
import ml_dtypes

BF16 = ml_dtypes.bfloat16


def bf(x):
    return np.asarray(x, np.float32).astype(BF16)


def f32(x):
    return np.asarray(x, np.float32)


def f64(x):
    return np.asarray(x).astype(np.float64)


def striped(idx):
    return np.tile(idx.reshape(-1, 16).T, (8, 1))


S, K, M, N, B, Q = 256, 128, 128, 256, 4, 64


def setup_inputs():
    return {"base": bf(np.random.standard_normal((B, M, S))), "x": bf(np.random.standard_normal((K, N))), "w": bf(np.random.standard_normal((K, M)) / np.sqrt(K)), "b": f32(0.5 * np.random.standard_normal((M, 1))), "offs": striped(np.random.permutation(S))}


def reference(base, x, w, b, offs):
    idx = offs[:16].T.reshape(-1)
    z = f64(base).copy()
    for i in range(B):
        z[i][:, idx[i * Q : (i + 1) * Q]] = f64(w).T @ f64(x)[:, i * Q : (i + 1) * Q]
    return np.tanh(z + f64(b))

@@ -1,0 +1,55 @@
+import concourse.mybir as mybir
+from concourse.masks import make_identity
+
+BF16, F32, U16 = mybir.dt.bfloat16, mybir.dt.float32, mybir.dt.uint16
+TANH = mybir.ActivationFunctionType.Tanh
+
+P = 128
+SEQS = 4
+TOKENS = 256
+PIECE = 64
+PIECE_COLS = PIECE // 16
+
+FLOPS = 2 * P * P * SEQS * PIECE
+
+
+def tile_scatter_matmul_kernel(tc, base, x, w, b, offs, out):
+    nc = tc.nc
+    with (
+        tc.tile_pool(name="held", bufs=1) as held,
+        tc.psum_pool(name="windows", bufs=1) as windows,
+    ):
+        offsets = held.tile([P, SEQS * PIECE_COLS], U16, name="offsets")
+        nc.sync.dma_start(offsets[:], offs)
+
+        base_sb = [held.tile([P, TOKENS], BF16, name=f"base_sb{i}") for i in range(SEQS)]
+        for i in range(SEQS):
+            nc.sync.dma_start(base_sb[i][:], base[i])
+
+        w_sb = held.tile([P, P], BF16, name="w_sb")
+        nc.scalar.dma_start(w_sb[:], w)
+        x_sb = held.tile([P, SEQS * PIECE], BF16, name="x_sb")
+        nc.scalar.dma_start(x_sb[:], x)
+        bias = held.tile([P, 1], F32, name="bias")
+        nc.scalar.dma_start(bias[:], b)
+
+        identity = held.tile([P, P], BF16, name="identity")
+        make_identity(nc, identity[:])
+
+        window = [windows.tile([P, TOKENS], F32, name=f"window{i}") for i in range(SEQS)]
+        for i in range(SEQS):
+            nc.tensor.matmul(window[i][:], identity[:], base_sb[i][:], start=True, stop=True)
+
+        for i in range(SEQS):
+            nc.tensor.matmul(
+                window[i][:].indirect(offsets[:, i * PIECE_COLS : (i + 1) * PIECE_COLS]),
+                w_sb[:],
+                x_sb[:, i * PIECE : (i + 1) * PIECE],
+                start=True,
+                stop=True,
+            )
+
+        for i in range(SEQS):
+            result = held.tile([P, TOKENS], F32, name=f"result{i}")
+            nc.scalar.activation(result[:], window[i][:], TANH, bias=bias[:])
+            nc.sync.dma_start(out[i], result[:])

@@ -36,6 +36,10 @@ def tile_scatter_matmul_kernel(tc, base, x, w, b, offs, out):
         identity = held.tile([P, P], BF16, name="identity")
         make_identity(nc, identity[:])
 
+        scratch = held.tile([P, 1], F32, name="scratch")
+        nc.vector.memset(scratch[:], 0.0)
+        nc.scalar.activation(scratch[:], scratch[:], TANH)
+
         window = [windows.tile([P, TOKENS], F32, name=f"window{i}") for i in range(SEQS)]
         for i in range(SEQS):
             nc.tensor.matmul(window[i][:], identity[:], base_sb[i][:], start=True, stop=True)

@@ -19,17 +19,18 @@ def tile_scatter_matmul_kernel(tc, base, x, w, b, offs, out):
         tc.tile_pool(name="held", bufs=1) as held,
         tc.psum_pool(name="windows", bufs=1) as windows,
     ):
-        offsets = held.tile([P, SEQS * PIECE_COLS], U16, name="offsets")
-        nc.sync.dma_start(offsets[:], offs)
-
         base_sb = [held.tile([P, TOKENS], BF16, name=f"base_sb{i}") for i in range(SEQS)]
         for i in range(SEQS):
-            nc.sync.dma_start(base_sb[i][:], base[i])
+            queue = nc.sync if i % 2 == 0 else nc.scalar
+            queue.dma_start(base_sb[i][:], base[i])
 
+        offsets = held.tile([P, SEQS * PIECE_COLS], U16, name="offsets")
+        nc.sync.dma_start(offsets[:], offs)
         w_sb = held.tile([P, P], BF16, name="w_sb")
         nc.scalar.dma_start(w_sb[:], w)
         x_sb = held.tile([P, SEQS * PIECE], BF16, name="x_sb")
-        nc.scalar.dma_start(x_sb[:], x)
+        nc.sync.dma_start(x_sb[:], x)
+
         bias = held.tile([P, 1], F32, name="bias")
         nc.scalar.dma_start(bias[:], b)
 

@@ -9,6 +9,8 @@ SEQS = 4
 TOKENS = 256
 PIECE = 64
 PIECE_COLS = PIECE // 16
+WARM_COLS = 256
+WARM_MATMULS = 4
 
 FLOPS = 2 * P * P * SEQS * PIECE
 
@@ -36,6 +38,12 @@ def tile_scatter_matmul_kernel(tc, base, x, w, b, offs, out):
 
         identity = held.tile([P, P], BF16, name="identity")
         make_identity(nc, identity[:])
+
+        zeros = held.tile([P, WARM_COLS], BF16, name="zeros")
+        nc.vector.memset(zeros[:], 0.0)
+        unread = windows.tile([P, WARM_COLS], F32, name="unread")
+        for r in range(WARM_MATMULS):
+            nc.tensor.matmul(unread[:], zeros[:, 0:P], zeros[:], start=True, stop=True)
 
         scratch = held.tile([P, 1], F32, name="scratch")
         nc.vector.memset(scratch[:], 0.0)

@@ -23,18 +23,17 @@ def tile_scatter_matmul_kernel(tc, base, x, w, b, offs, out):
     ):
         base_sb = [held.tile([P, TOKENS], BF16, name=f"base_sb{i}") for i in range(SEQS)]
         for i in range(SEQS):
-            queue = nc.sync if i % 2 == 0 else nc.scalar
-            queue.dma_start(base_sb[i][:], base[i])
+            nc.sync.dma_start(base_sb[i][:], base[i])
 
         offsets = held.tile([P, SEQS * PIECE_COLS], U16, name="offsets")
         nc.sync.dma_start(offsets[:], offs)
         w_sb = held.tile([P, P], BF16, name="w_sb")
-        nc.scalar.dma_start(w_sb[:], w)
+        nc.sync.dma_start(w_sb[:], w)
         x_sb = held.tile([P, SEQS * PIECE], BF16, name="x_sb")
         nc.sync.dma_start(x_sb[:], x)
 
         bias = held.tile([P, 1], F32, name="bias")
-        nc.scalar.dma_start(bias[:], b)
+        nc.sync.dma_start(bias[:], b)
 
         identity = held.tile([P, P], BF16, name="identity")
         make_identity(nc, identity[:])

@@ -9,6 +9,7 @@ SEQS = 4
 TOKENS = 256
 PIECE = 64
 PIECE_COLS = PIECE // 16
+BLOCK = 32
 WARM_COLS = 256
 WARM_MATMULS = 4
 
@@ -32,8 +33,13 @@ def tile_scatter_matmul_kernel(tc, base, x, w, b, offs, out):
         x_sb = held.tile([P, SEQS * PIECE], BF16, name="x_sb")
         nc.sync.dma_start(x_sb[:], x)
 
-        bias = held.tile([P, 1], F32, name="bias")
-        nc.sync.dma_start(bias[:], b)
+        bias_rows = held.tile([P, BLOCK], F32, name="bias_rows", align_bytes=64)
+        nc.vector.memset(bias_rows[:], 0.0)
+        nc.scalar.dma_start(bias_rows[0:P:BLOCK, :], b.rearrange("(q c) o -> q (c o)", c=BLOCK))
+
+        bias_cols = held.tile([P, BLOCK], F32, name="bias_cols", align_bytes=64)
+        nc.vector.transpose(bias_cols[:], bias_rows[:])
+        bias = bias_cols[:, 0:1]
 
         identity = held.tile([P, P], BF16, name="identity")
         make_identity(nc, identity[:])
@@ -63,5 +69,5 @@ def tile_scatter_matmul_kernel(tc, base, x, w, b, offs, out):
 
         for i in range(SEQS):
             result = held.tile([P, TOKENS], F32, name=f"result{i}")
-            nc.scalar.activation(result[:], window[i][:], TANH, bias=bias[:])
+            nc.scalar.activation(result[:], window[i][:], TANH, bias=bias)
             nc.sync.dma_start(out[i], result[:])

@@ -69,5 +69,8 @@ def tile_scatter_matmul_kernel(tc, base, x, w, b, offs, out):
 
         for i in range(SEQS):
             result = held.tile([P, TOKENS], F32, name=f"result{i}")
-            nc.scalar.activation(result[:], window[i][:], TANH, bias=bias)
-            nc.sync.dma_start(out[i], result[:])
+            width = TOKENS // 2 if i == 0 else TOKENS
+            for first in range(0, TOKENS, width):
+                cols = slice(first, first + width)
+                nc.scalar.activation(result[:, cols], window[i][:, cols], TANH, bias=bias)
+                nc.sync.dma_start(out[i][:, cols], result[:, cols])

@@ -23,15 +23,16 @@ def tile_scatter_matmul_kernel(tc, base, x, w, b, offs, out):
         tc.psum_pool(name="windows", bufs=1) as windows,
     ):
         base_sb = [held.tile([P, TOKENS], BF16, name=f"base_sb{i}") for i in range(SEQS)]
-        for i in range(SEQS):
+        for i in (0, 1):
             nc.sync.dma_start(base_sb[i][:], base[i])
-
         offsets = held.tile([P, SEQS * PIECE_COLS], U16, name="offsets")
         nc.sync.dma_start(offsets[:], offs)
         w_sb = held.tile([P, P], BF16, name="w_sb")
         nc.sync.dma_start(w_sb[:], w)
         x_sb = held.tile([P, SEQS * PIECE], BF16, name="x_sb")
         nc.sync.dma_start(x_sb[:], x)
+        for i in (2, 3):
+            nc.sync.dma_start(base_sb[i][:], base[i])
 
         bias_rows = held.tile([P, BLOCK], F32, name="bias_rows", align_bytes=64)
         nc.vector.memset(bias_rows[:], 0.0)
@@ -55,17 +56,21 @@ def tile_scatter_matmul_kernel(tc, base, x, w, b, offs, out):
         nc.scalar.activation(scratch[:], scratch[:], TANH)
 
         window = [windows.tile([P, TOKENS], F32, name=f"window{i}") for i in range(SEQS)]
-        for i in range(SEQS):
-            nc.tensor.matmul(window[i][:], identity[:], base_sb[i][:], start=True, stop=True)
-
-        for i in range(SEQS):
-            nc.tensor.matmul(
-                window[i][:].indirect(offsets[:, i * PIECE_COLS : (i + 1) * PIECE_COLS]),
-                w_sb[:],
-                x_sb[:, i * PIECE : (i + 1) * PIECE],
-                start=True,
-                stop=True,
-            )
+        fill_matmuls = {0: 1, 1: 1, 2: 16, 3: 8}
+        for pair in ((0, 1), (2, 3)):
+            for i in pair:
+                width = TOKENS // fill_matmuls[i]
+                for first in range(0, TOKENS, width):
+                    cols = slice(first, first + width)
+                    nc.tensor.matmul(window[i][:, cols], identity[:], base_sb[i][:, cols], start=True, stop=True)
+            for i in pair:
+                nc.tensor.matmul(
+                    window[i][:].indirect(offsets[:, i * PIECE_COLS : (i + 1) * PIECE_COLS]),
+                    w_sb[:],
+                    x_sb[:, i * PIECE : (i + 1) * PIECE],
+                    start=True,
+                    stop=True,
+                )
 
         for i in range(SEQS):
             result = held.tile([P, TOKENS], F32, name=f"result{i}")

@@ -55,22 +55,34 @@ def tile_scatter_matmul_kernel(tc, base, x, w, b, offs, out):
         nc.vector.memset(scratch[:], 0.0)
         nc.scalar.activation(scratch[:], scratch[:], TANH)
 
+        def scatter(i):
+            nc.tensor.matmul(
+                window[i][:].indirect(offsets[:, i * PIECE_COLS : (i + 1) * PIECE_COLS]),
+                w_sb[:],
+                x_sb[:, i * PIECE : (i + 1) * PIECE],
+                start=True,
+                stop=True,
+            )
+
         window = [windows.tile([P, TOKENS], F32, name=f"window{i}") for i in range(SEQS)]
-        fill_matmuls = {0: 1, 1: 1, 2: 16, 3: 8}
-        for pair in ((0, 1), (2, 3)):
-            for i in pair:
-                width = TOKENS // fill_matmuls[i]
-                for first in range(0, TOKENS, width):
-                    cols = slice(first, first + width)
-                    nc.tensor.matmul(window[i][:, cols], identity[:], base_sb[i][:, cols], start=True, stop=True)
-            for i in pair:
-                nc.tensor.matmul(
-                    window[i][:].indirect(offsets[:, i * PIECE_COLS : (i + 1) * PIECE_COLS]),
-                    w_sb[:],
-                    x_sb[:, i * PIECE : (i + 1) * PIECE],
-                    start=True,
-                    stop=True,
-                )
+        for i in (0, 1):
+            nc.tensor.matmul(window[i][:], identity[:], base_sb[i][:], start=True, stop=True)
+        scatter(0)
+        scatter(1)
+        for i, pieces in ((2, 4), (3, 2)):
+            width = TOKENS // pieces
+            for first in range(0, TOKENS, width):
+                cols = slice(first, first + width)
+                for f in range(0, P, BLOCK):
+                    nc.tensor.matmul(
+                        window[i][f : f + BLOCK, cols],
+                        identity[:, f : f + BLOCK],
+                        base_sb[i][:, cols],
+                        start=True,
+                        stop=True,
+                    )
+        scatter(2)
+        scatter(3)
 
         for i in range(SEQS):
             result = held.tile([P, TOKENS], F32, name=f"result{i}")

@@ -10,8 +10,8 @@ TOKENS = 256
 PIECE = 64
 PIECE_COLS = PIECE // 16
 BLOCK = 32
-WARM_COLS = 256
-WARM_MATMULS = 4
+WARM_COLS = 128
+WARM_MATMULS = 10
 
 FLOPS = 2 * P * P * SEQS * PIECE
 
@@ -22,6 +22,13 @@ def tile_scatter_matmul_kernel(tc, base, x, w, b, offs, out):
         tc.tile_pool(name="held", bufs=1) as held,
         tc.psum_pool(name="windows", bufs=1) as windows,
     ):
+        zeros = held.tile([P, WARM_COLS // 2], F32, name="zeros")
+        nc.vector.memset(zeros[:], 0.0)
+        zeros_bf16 = zeros[:].bitcast(BF16)
+        unread = windows.tile([P, WARM_COLS], F32, name="unread")
+        for r in range(WARM_MATMULS):
+            nc.tensor.matmul(unread[:], zeros_bf16, zeros_bf16, start=True, stop=True)
+
         base_sb = [held.tile([P, TOKENS], BF16, name=f"base_sb{i}") for i in range(SEQS)]
         for i in (0, 1):
             nc.sync.dma_start(base_sb[i][:], base[i])
@@ -35,7 +42,7 @@ def tile_scatter_matmul_kernel(tc, base, x, w, b, offs, out):
             nc.sync.dma_start(base_sb[i][:], base[i])
 
         bias_rows = held.tile([P, BLOCK], F32, name="bias_rows", align_bytes=64)
-        nc.vector.memset(bias_rows[:], 0.0)
+        nc.gpsimd.memset(bias_rows[:], 0.0)
         nc.scalar.dma_start(bias_rows[0:P:BLOCK, :], b.rearrange("(q c) o -> q (c o)", c=BLOCK))
 
         bias_cols = held.tile([P, BLOCK], F32, name="bias_cols", align_bytes=64)
@@ -44,12 +51,6 @@ def tile_scatter_matmul_kernel(tc, base, x, w, b, offs, out):
 
         identity = held.tile([P, P], BF16, name="identity")
         make_identity(nc, identity[:])
-
-        zeros = held.tile([P, WARM_COLS], BF16, name="zeros")
-        nc.vector.memset(zeros[:], 0.0)
-        unread = windows.tile([P, WARM_COLS], F32, name="unread")
-        for r in range(WARM_MATMULS):
-            nc.tensor.matmul(unread[:], zeros[:, 0:P], zeros[:], start=True, stop=True)
 
         scratch = held.tile([P, 1], F32, name="scratch")
         nc.vector.memset(scratch[:], 0.0)

import concourse.mybir as mybir
from concourse.masks import make_identity

BF16, F32, U16 = mybir.dt.bfloat16, mybir.dt.float32, mybir.dt.uint16
TANH = mybir.ActivationFunctionType.Tanh

P = 128
SEQS = 4
TOKENS = 256
PIECE = 64
PIECE_COLS = PIECE // 16
BLOCK = 32
WARM_COLS = 128
WARM_MATMULS = 10

FLOPS = 2 * P * P * SEQS * PIECE


def tile_scatter_matmul_kernel(tc, base, x, w, b, offs, out):
    nc = tc.nc
    with (
        tc.tile_pool(name="held", bufs=1) as held,
        tc.psum_pool(name="windows", bufs=1) as windows,
    ):
        zeros = held.tile([P, WARM_COLS // 2], F32, name="zeros")
        nc.vector.memset(zeros[:], 0.0)
        zeros_bf16 = zeros[:].bitcast(BF16)
        unread = windows.tile([P, WARM_COLS], F32, name="unread")
        for r in range(WARM_MATMULS):
            nc.tensor.matmul(unread[:], zeros_bf16, zeros_bf16, start=True, stop=True)

        base_sb = [held.tile([P, TOKENS], BF16, name=f"base_sb{i}") for i in range(SEQS)]
        for i in (0, 1):
            nc.sync.dma_start(base_sb[i][:], base[i])
        offsets = held.tile([P, SEQS * PIECE_COLS], U16, name="offsets")
        nc.sync.dma_start(offsets[:], offs)
        w_sb = held.tile([P, P], BF16, name="w_sb")
        nc.sync.dma_start(w_sb[:], w)
        x_sb = held.tile([P, SEQS * PIECE], BF16, name="x_sb")
        nc.sync.dma_start(x_sb[:], x)
        for i in (2, 3):
            nc.sync.dma_start(base_sb[i][:], base[i])

        bias_rows = held.tile([P, BLOCK], F32, name="bias_rows", align_bytes=64)
        nc.gpsimd.memset(bias_rows[:], 0.0)
        nc.scalar.dma_start(bias_rows[0:P:BLOCK, :], b.rearrange("(q c) o -> q (c o)", c=BLOCK))

        bias_cols = held.tile([P, BLOCK], F32, name="bias_cols", align_bytes=64)
        nc.vector.transpose(bias_cols[:], bias_rows[:])
        bias = bias_cols[:, 0:1]

        identity = held.tile([P, P], BF16, name="identity")
        make_identity(nc, identity[:])

        scratch = held.tile([P, 1], F32, name="scratch")
        nc.vector.memset(scratch[:], 0.0)
        nc.scalar.activation(scratch[:], scratch[:], TANH)

        def scatter(i):
            nc.tensor.matmul(
                window[i][:].indirect(offsets[:, i * PIECE_COLS : (i + 1) * PIECE_COLS]),
                w_sb[:],
                x_sb[:, i * PIECE : (i + 1) * PIECE],
                start=True,
                stop=True,
            )

        window = [windows.tile([P, TOKENS], F32, name=f"window{i}") for i in range(SEQS)]
        for i in (0, 1):
            nc.tensor.matmul(window[i][:], identity[:], base_sb[i][:], start=True, stop=True)
        scatter(0)
        scatter(1)
        for i, pieces in ((2, 4), (3, 2)):
            width = TOKENS // pieces
            for first in range(0, TOKENS, width):
                cols = slice(first, first + width)
                for f in range(0, P, BLOCK):
                    nc.tensor.matmul(
                        window[i][f : f + BLOCK, cols],
                        identity[:, f : f + BLOCK],
                        base_sb[i][:, cols],
                        start=True,
                        stop=True,
                    )
        scatter(2)
        scatter(3)

        for i in range(SEQS):
            result = held.tile([P, TOKENS], F32, name=f"result{i}")
            width = TOKENS // 2 if i == 0 else TOKENS
            for first in range(0, TOKENS, width):
                cols = slice(first, first + width)
                nc.scalar.activation(result[:, cols], window[i][:, cols], TANH, bias=bias)
                nc.sync.dma_start(out[i][:, cols], result[:, cols])
